import numpy as np
import ml_dtypes


def mxq(x, axis, fmt="e4m3"):
    dtype, down = {"e4m3": (ml_dtypes.float8_e4m3fn, 7), "e5m2": (ml_dtypes.float8_e5m2, 14)}[fmt]
    v = np.moveaxis(np.asarray(x, np.float32).astype(ml_dtypes.bfloat16).astype(np.float64), axis, -1)
    blocks = v.reshape(v.shape[:-1] + (-1, 32))
    amax = np.abs(blocks).max(-1, keepdims=True)
    byte = np.maximum(np.where(amax > 0, np.frexp(amax)[1] - 1 + 127, 0) - down, 1)
    scale = np.exp2(byte - 127.0)
    codes = (blocks / scale).astype(np.float32).astype(dtype).astype(np.float64)
    return np.moveaxis((codes * scale).reshape(v.shape), -1, axis)


WIDE = False


def mx_kscale(k):
    if not WIDE:
        return np.ones(k)
    levels = np.array([10, -10, 5, -5, 0])
    if k % 512:
        return np.exp2(np.random.permutation(np.resize(levels, k // 32))).repeat(32)
    a = np.empty((k // 512, 16))
    for p in range(k // 512):
        a[p, :8] = np.random.permutation(np.resize(levels, 8))
        for g in range(8):
            far = levels[np.abs(levels - a[p, g]) >= 10]
            a[p, g + 8] = far[np.random.randint(len(far))]
    return np.exp2(a.ravel()).repeat(32)


BF16 = ml_dtypes.bfloat16


def bf(x):
    return np.asarray(x, np.float32).astype(BF16)


def f64(x):
    return np.asarray(x).astype(np.float64)


E2M1 = np.array([0.0, 0.5, 1.0, 1.5, 2.0, 3.0, 4.0, 6.0, -0.0, -0.5, -1.0, -1.5, -2.0, -3.0, -4.0, -6.0])


def pack_weight(w, fmt):
    k, n = w.shape
    w = f64(bf(w)).reshape(k // 32, 32, n)
    amax = np.abs(w).max(1)
    if fmt == "e4m3":
        byte = np.frexp(amax)[1] - 1 + 127 - 7
    else:
        mant, ex = np.frexp(amax / 6.0)
        byte = np.where(mant > 0.5, ex, ex - 1) + 127
    byte = np.clip(np.where(amax > 0, byte, 1), 1, 254)
    scaled = (w * np.exp2(127.0 - byte)[:, None, :]).reshape(k, n).astype(np.float32)
    by_word = np.ascontiguousarray(scaled.reshape(k // 512, 128, 4, n).transpose(0, 1, 3, 2))
    if fmt == "e4m3":
        words = by_word.astype(ml_dtypes.float8_e4m3fn).view(np.uint8)
    else:
        c = by_word.astype(ml_dtypes.float4_e2m1fn).view(np.uint8) & 0xF
        words = c[..., 0::2] | (c[..., 1::2] << 4)
    return np.ascontiguousarray(words), np.ascontiguousarray(byte.astype(np.uint8).reshape(k // 512, 16, n))


def unpack_weight(words, scales, fmt):
    g, p, n, _ = words.shape
    if fmt == "e4m3":
        vals = np.ascontiguousarray(words).view(ml_dtypes.float8_e4m3fn).astype(np.float64)
    else:
        nib = np.empty((g, p, n, 4), np.uint8)
        nib[..., 0::2] = words & 0xF
        nib[..., 1::2] = words >> 4
        vals = E2M1[nib]
    vals = vals * np.repeat(np.exp2(scales.astype(np.float64) - 127.0), 8, axis=1)[..., None]
    return vals.transpose(0, 1, 3, 2).reshape(g * 512, n)
def pack4(w):
    words, scales = pack_weight(w, "e2m1")
    return words.reshape(words.shape[0], 128, -1), scales


def unpack4(words, scales):
    return unpack_weight(words.reshape(words.shape[0], 128, -1, 2), scales, "e2m1")


E4M3FN = np.array([(-1.0 if i & 128 else 1.0) * ((1.0 + (i & 7) / 8.0) * 2.0 ** (((i >> 3) & 15) - 7) if i & 120 else (i & 7) * 2.0 ** -9) for i in range(256)])


def e4m3fn_bytes(y):
    return np.clip(np.asarray(y, np.float64), -448.0, 448.0).astype(np.float32).astype(ml_dtypes.float8_e4m3fn).view(np.uint8)


def e4m3fn_values(b):
    return E4M3FN[b]


C, N, E, L = 1024, 1024, 8, 512


def setup_inputs():
    s = mx_kscale(C)
    offset = 0.5 * np.random.standard_normal((C, E, 1))
    X = (np.random.standard_normal((C, E, L)) + offset).reshape(C, E * L) * s[:, None]
    X_scale = (np.abs(X).max(axis=1, keepdims=True) / 448).astype(np.float32)
    X_bytes = e4m3fn_bytes(X / f64(X_scale))
    W_words, W_scales = pack4(np.random.standard_normal((C, N)) / np.sqrt(C) / s[:, None])
    return {"X_bytes": X_bytes, "X_scale": X_scale,
            "W_words": W_words, "W_scales": W_scales,
            "gain": bf(1 + 0.1 * np.random.standard_normal(N))}


def reference(X_bytes, X_scale, W_words, W_scales, gain):
    X = e4m3fn_values(X_bytes) * np.repeat(f64(X_scale), E * L, axis=1)
    W = unpack4(W_words, W_scales)
    Y = W.T @ mxq(X, 0, "e4m3")
    Y = Y.reshape(N, E, L)
    centred = Y - Y.mean(axis=2, keepdims=True)
    S = centred * f64(gain)[:, None, None]
    return S.reshape(N, E * L)

from contextlib import ExitStack

import concourse.mybir as mybir
from concourse.masks import make_identity

C, N, E, L = 1024, 1024, 8, 512
FLOPS = 2 * C * N * E * L

F32 = mybir.dt.float32
BF16 = mybir.dt.bfloat16
I32 = mybir.dt.int32
U32 = mybir.dt.uint32
U8 = mybir.dt.uint8
FP8 = mybir.dt.float8_e4m3fn
FP8X4 = mybir.dt.float8_e4m3fn_x4
FP4X4 = mybir.dt.float4_e2m1fn_x4
ALU = mybir.AluOpType
ACT = mybir.ActivationFunctionType

P = 128
PACK = 4
G = C // (P * PACK)
J = N // P
PIECES = E * G
LOAD_EPOCHS = [(0, 1), (1, 2), (2, 4), (4, 8)]
VECTOR_PLANES = [3, 1, 0, 3, 2, 2, 2, 2, 2, 2, 2, 2, 2, 2, 2, 1]
RUN = 4


def tile_eeg_epoch_unmixing_d6_kernel(tc, X_bytes, X_scale, W_words, W_scales, gain, out):
    nc = tc.nc
    with ExitStack() as ctx:
        keep = ctx.enter_context(tc.tile_pool(name="keep", bufs=1))
        stage = ctx.enter_context(tc.tile_pool(name="stage", bufs=3))
        psum = ctx.enter_context(tc.psum_pool(name="psum", bufs=8))
        ctx.enter_context(tc.manual_schedule())

        x_scale = keep.tile([P, G, PACK], F32, name="x_scale")
        w_words = keep.tile([P, G, 2 * N], U8, name="w_words", align_bytes=64)
        w_scales = keep.tile([P, G, N], U8, name="w_scales", align_bytes=64)
        gain_rows = keep.tile([P, P], BF16, name="gain_rows")
        ident = keep.tile([P, P], BF16, name="ident")
        factor = keep.tile([P, J], F32, name="factor")
        means = keep.tile([P, E * J], F32, name="means")
        warm = keep.tile([P, 2], F32, name="warm")

        nc.vector.memset(gain_rows[:].bitcast(I32), 0)
        nc.vector.memset(w_scales[:].rearrange("p g n -> p (g n)").bitcast(I32), 0)
        nc.vector.memset(warm[:, 0:1], 0.0)
        nc.scalar.activation(out=warm[:, 1:2], in_=warm[:, 0:1], func=ACT.Copy)
        make_identity(nc, ident[:])

        x_view = X_bytes.rearrange("(g p t) s -> g p t s", p=P, t=PACK)
        x_src = {}

        def load_x(chunk):
            first, last = LOAD_EPOCHS[chunk]
            for g in range(G):
                x_bytes = keep.tile([P, PACK, (last - first) * L], U8, name="x_bytes_%d_%d" % (chunk, g))
                nc.sync.dma_start(out=x_bytes[:], in_=x_view[g][:, :, first * L : last * L])
                for e in range(first, last):
                    x_src[G * e + g] = (x_bytes, (e - first) * L)

        nc.sync.dma_start(out=x_scale[:], in_=X_scale.rearrange("(g p t) o -> p g (t o)", p=P, t=PACK))
        load_x(0)
        load_x(1)
        nc.sync.dma_start(out=w_words[:].bitcast(I32), in_=W_words.rearrange("g p n -> p g n").bitcast(I32))
        nc.sync.dma_start(out=gain_rows[0:J, :], in_=gain.rearrange("(j p) -> j p", p=P))
        for q in range(4):
            nc.sync.dma_start(
                out=w_scales[32 * q : 32 * q + 4, :, :].bitcast(I32),
                in_=W_scales[:, 4 * q : 4 * q + 4, :].rearrange("g r n -> r g n").bitcast(I32),
            )
        load_x(2)
        load_x(3)

        planes, grouped, codes, scales, result = {}, {}, {}, {}, {}

        def widen(piece, t, on_vector):
            if piece not in planes:
                planes[piece] = stage.tile([P, PACK, L], BF16, name="planes", bufs=4)
            x_bytes, col = x_src[piece]
            g = piece % G
            src = x_bytes[:, t, col : col + L].bitcast(FP8)
            if on_vector:
                nc.vector.tensor_scalar(out=planes[piece][:, t, :], in0=src, scalar1=x_scale[:, g, t : t + 1],
                                        scalar2=None, op0=ALU.mult)
            else:
                nc.scalar.activation(out=planes[piece][:, t, :], in_=src, func=ACT.Copy,
                                     scale=x_scale[:, g, t : t + 1])

        def interleave(piece):
            if piece < PIECES:
                grouped[piece] = stage.tile([P, L, PACK], BF16, name="grouped", align_bytes=64)
                nc.vector.tensor_copy(
                    out=grouped[piece][:].rearrange("p (c i) t -> p c t i", i=RUN),
                    in_=planes[piece][:].rearrange("p t (c i) -> p c t i", i=RUN),
                )

        def quantize(piece):
            if piece < PIECES:
                codes[piece] = stage.tile([P, L], U32, name="codes", align_bytes=64, bufs=5)
                scales[piece] = stage.tile([P, L], U8, name="scales", align_bytes=64, bufs=5)
                nc.vector.quantize_mx(out=codes[piece][:].bitcast(FP8X4), scales=scales[piece][:],
                                      in_=grouped[piece][:].rearrange("p c t -> p (c t)"))

        def multiply_and_empty(n):
            e, j = divmod(n, J)
            acc = psum.tile([P, L], F32, name="acc")
            for g in range(G):
                nc.tensor.matmul_mx(
                    out=acc[:],
                    lhsT=w_words[:, g, 2 * P * j : 2 * P * (j + 1)].bitcast(FP4X4),
                    lhsT_scale=w_scales[:, g, P * j : P * (j + 1)],
                    rhs=codes[G * e + g][:].bitcast(FP8X4),
                    rhs_scale=scales[G * e + g][:],
                    start=(g == 0),
                    stop=(g == G - 1),
                )
            result[n] = stage.tile([P, L], F32, name="result", bufs=24)
            nc.scalar.activation(out=result[n][:], in_=acc[:], func=ACT.Copy, scale=factor[:, j : j + 1],
                                 accum_out=means[:, n : n + 1])

        def centre_and_store(n):
            if n >= 0:
                e, j = divmod(n, J)
                nc.vector.tensor_scalar(out=result[n][:], in0=result[n][:], scalar1=float(L),
                                        scalar2=means[:, n : n + 1], op0=ALU.mult, op1=ALU.subtract)
                nc.sync.dma_start(out=out[P * j : P * (j + 1), L * e : L * (e + 1)], in_=result[n][:])

        def shares(piece):
            if piece >= PIECES:
                return [], []
            cut = PACK - VECTOR_PLANES[piece]
            return list(range(cut)), list(range(cut, PACK))

        for piece in (0, 1, 2):
            for t in shares(piece)[0]:
                widen(piece, t, False)
        for t in shares(0)[1]:
            widen(0, t, True)
        gain_cols = psum.tile([P, L], F32, name="acc")
        nc.tensor.matmul(out=gain_cols[:, 0:J], lhsT=gain_rows[:], rhs=ident[:, 0:J], start=True, stop=True)
        interleave(0)
        for t in shares(1)[1]:
            widen(1, t, True)
        quantize(0)
        interleave(1)
        nc.vector.tensor_scalar(out=factor[:], in0=gain_cols[:, 0:J], scalar1=1.0 / L, scalar2=None, op0=ALU.mult)
        for t in shares(2)[1]:
            widen(2, t, True)
        quantize(1)

        for h in range(PIECES):
            on_scalar, on_vector = shares(h + 3)
            interleave(h + 2)
            centre_and_store(4 * h - 1)
            quantize(h + 2)
            for i in range(4):
                multiply_and_empty(4 * h + i)
                if on_scalar:
                    widen(h + 3, on_scalar.pop(0), False)
                if i > 0 and on_vector:
                    widen(h + 3, on_vector.pop(0), True)
                if i < 3:
                    centre_and_store(4 * h + i)
            for t in on_vector:
                widen(h + 3, t, True)
        centre_and_store(E * J - 1)
